import numpy as np
import ml_dtypes


def mxq(x, axis, fmt="e4m3"):
    dtype, down = {"e4m3": (ml_dtypes.float8_e4m3fn, 7), "e5m2": (ml_dtypes.float8_e5m2, 14)}[fmt]
    v = np.moveaxis(np.asarray(x, np.float32).astype(ml_dtypes.bfloat16).astype(np.float64), axis, -1)
    blocks = v.reshape(v.shape[:-1] + (-1, 32))
    amax = np.abs(blocks).max(-1, keepdims=True)
    byte = np.maximum(np.where(amax > 0, np.frexp(amax)[1] - 1 + 127, 0) - down, 1)
    scale = np.exp2(byte - 127.0)
    codes = (blocks / scale).astype(np.float32).astype(dtype).astype(np.float64)
    return np.moveaxis((codes * scale).reshape(v.shape), -1, axis)


WIDE = False


def mx_kscale(k):
    if not WIDE:
        return np.ones(k)
    levels = np.array([10, -10, 5, -5, 0])
    if k % 512:
        return np.exp2(np.random.permutation(np.resize(levels, k // 32))).repeat(32)
    a = np.empty((k // 512, 16))
    for p in range(k // 512):
        a[p, :8] = np.random.permutation(np.resize(levels, 8))
        for g in range(8):
            far = levels[np.abs(levels - a[p, g]) >= 10]
            a[p, g + 8] = far[np.random.randint(len(far))]
    return np.exp2(a.ravel()).repeat(32)


BF16 = ml_dtypes.bfloat16


def bf(x):
    return np.asarray(x, np.float32).astype(BF16)


def f64(x):
    return np.asarray(x).astype(np.float64)


E2M1 = np.array([0.0, 0.5, 1.0, 1.5, 2.0, 3.0, 4.0, 6.0, -0.0, -0.5, -1.0, -1.5, -2.0, -3.0, -4.0, -6.0])


def pack_weight(w, fmt):
    k, n = w.shape
    w = f64(bf(w)).reshape(k // 32, 32, n)
    amax = np.abs(w).max(1)
    if fmt == "e4m3":
        byte = np.frexp(amax)[1] - 1 + 127 - 7
    else:
        mant, ex = np.frexp(amax / 6.0)
        byte = np.where(mant > 0.5, ex, ex - 1) + 127
    byte = np.clip(np.where(amax > 0, byte, 1), 1, 254)
    scaled = (w * np.exp2(127.0 - byte)[:, None, :]).reshape(k, n).astype(np.float32)
    by_word = np.ascontiguousarray(scaled.reshape(k // 512, 128, 4, n).transpose(0, 1, 3, 2))
    if fmt == "e4m3":
        words = by_word.astype(ml_dtypes.float8_e4m3fn).view(np.uint8)
    else:
        c = by_word.astype(ml_dtypes.float4_e2m1fn).view(np.uint8) & 0xF
        words = c[..., 0::2] | (c[..., 1::2] << 4)
    return np.ascontiguousarray(words), np.ascontiguousarray(byte.astype(np.uint8).reshape(k // 512, 16, n))


def unpack_weight(words, scales, fmt):
    g, p, n, _ = words.shape
    if fmt == "e4m3":
        vals = np.ascontiguousarray(words).view(ml_dtypes.float8_e4m3fn).astype(np.float64)
    else:
        nib = np.empty((g, p, n, 4), np.uint8)
        nib[..., 0::2] = words & 0xF
        nib[..., 1::2] = words >> 4
        vals = E2M1[nib]
    vals = vals * np.repeat(np.exp2(scales.astype(np.float64) - 127.0), 8, axis=1)[..., None]
    return vals.transpose(0, 1, 3, 2).reshape(g * 512, n)
def pack4(w):
    words, scales = pack_weight(w, "e2m1")
    return words.reshape(words.shape[0], 128, -1), scales


def unpack4(words, scales):
    return unpack_weight(words.reshape(words.shape[0], 128, -1, 2), scales, "e2m1")


M, A, B, L, R = 1024, 512, 1024, 2048, 512


def draw0():
    s, u, t = mx_kscale(A), mx_kscale(B), mx_kscale(L)
    z_rest = 0.5 * np.random.standard_normal((B, L)) / np.sqrt(B) / u[:, None]
    alpha = np.random.standard_normal((L, R)) / np.sqrt(L) / t[:, None]
    z_rest_words, z_rest_scales = pack4(z_rest)
    alpha_words, alpha_scales = pack4(alpha)
    return {"x_top": bf(np.random.standard_normal((M, A)) * s),
            "x_rest": bf(np.random.standard_normal((M, B)) * u),
            "z_top": bf(0.5 * np.random.standard_normal((L, A)) / np.sqrt(A) / s),
            "z_rest_words": z_rest_words, "z_rest_scales": z_rest_scales,
            "landmark_gain": bf((1 + 0.1 * np.random.standard_normal(L)) * t),
            "query_gain": bf(1 + 0.1 * np.random.standard_normal(M)),
            "alpha_words": alpha_words, "alpha_scales": alpha_scales,
            "intercept": bf(0.3 * np.random.standard_normal(R))}


def core(x_top, x_rest, z_top, z_rest_words, z_rest_scales, landmark_gain, query_gain,
              alpha_words, alpha_scales, intercept):
    z_rest = unpack4(z_rest_words, z_rest_scales)
    alpha = unpack4(alpha_words, alpha_scales)
    top = mxq(f64(x_top), 1, "e4m3") @ mxq(f64(z_top), 1, "e4m3").T
    rest = mxq(f64(x_rest), 1, "e4m3") @ z_rest
    kern = np.exp(top + rest) * f64(landmark_gain)
    pred = mxq(kern, 1, "e4m3") @ alpha
    return pred * f64(query_gain)[:, None] + f64(intercept)


def e4m3fn_bytes(y):
    return np.clip(np.asarray(y, np.float64), -448.0, 448.0).astype(np.float32).astype(ml_dtypes.float8_e4m3fn).view(np.uint8)


def e4m3fn_values(b):
    return np.asarray(b, np.uint8).view(ml_dtypes.float8_e4m3fn).astype(np.float64)


def setup_inputs():
    d = draw0()
    x0 = np.asarray(d['z_top']).astype(np.float64)
    s = (np.max(np.abs(x0), axis=(0,), keepdims=True) / 448.0).astype(np.float32)
    out = {}
    for k, v in d.items():
        if k == 'z_top':
            out['z_top_bytes'] = e4m3fn_bytes(x0 / s.astype(np.float64))
            out['z_top_scale'] = s
        else:
            out[k] = v
    return out


def reference(x_top, x_rest, z_top_bytes, z_top_scale, z_rest_words, z_rest_scales, landmark_gain, query_gain, alpha_words, alpha_scales, intercept):
    return core(x_top, x_rest, e4m3fn_values(z_top_bytes) * z_top_scale.astype(np.float64), z_rest_words, z_rest_scales, landmark_gain, query_gain, alpha_words, alpha_scales, intercept)

@@ -1,0 +1,280 @@
+from contextlib import ExitStack
+
+import concourse.mybir as mybir
+from concourse.masks import make_identity
+
+M, A, B, L, R = 1024, 512, 1024, 2048, 512
+FLOPS = 2 * M * (A + B) * L + 2 * M * L * R
+
+F32 = mybir.dt.float32
+BF16 = mybir.dt.bfloat16
+U32 = mybir.dt.uint32
+I32 = mybir.dt.int32
+U8 = mybir.dt.uint8
+FP8 = mybir.dt.float8_e4m3fn
+FP8X4 = mybir.dt.float8_e4m3fn_x4
+FP4X4 = mybir.dt.float4_e2m1fn_x4
+ALU = mybir.AluOpType
+ACT = mybir.ActivationFunctionType
+
+P = 128
+NC = L // 512
+NH = 2
+MH = M // NH
+RT = MH // P
+SPLIT = 192
+
+
+def tile_landmark_kernel_ridge_s3_kernel(
+    tc, x_top, x_rest, z_top_bytes, z_top_scale, z_rest_words, z_rest_scales,
+    landmark_gain, query_gain, alpha_words, alpha_scales, intercept, out,
+):
+    nc = tc.nc
+    with ExitStack() as ctx:
+        keep = ctx.enter_context(tc.tile_pool(name="keep", bufs=1))
+        psum = ctx.enter_context(tc.psum_pool(name="psum", bufs=4))
+
+        def alloc(name, shape, dtype, bufs=1):
+            return keep.tile(shape, dtype, name=name, bufs=bufs, align_bytes=64)
+
+        def bank(name):
+            return psum.tile([P, 512], F32, name=name)
+
+        sc4 = alloc("sc4", [P, 4], F32)
+        gain = alloc("gain", [P, NC, 4], BF16)
+        qg = alloc("qg", [P, 8], BF16)
+        ic4 = alloc("ic4", [P, 4], BF16)
+        nc.scalar.dma_start(out=sc4[:], in_=z_top_scale.rearrange("o (p q) -> p (o q)", q=4))
+        nc.scalar.dma_start(out=gain[:], in_=landmark_gain.rearrange("(c j t) -> j c t", c=NC, t=4))
+        nc.gpsimd.dma_start(out=qg[:], in_=query_gain.rearrange("(p i) -> p i", i=8))
+        nc.gpsimd.dma_start(out=ic4[:], in_=intercept.rearrange("(p q) -> p q", q=4))
+
+        zs_raw = alloc("zs_raw", [P, 2, L], U8)
+        cs = alloc("cs", [P, NC, R], U8)
+        nc.vector.memset(zs_raw[:].bitcast(I32), 0)
+        nc.vector.memset(cs[:].bitcast(I32), 0)
+
+        x_top_v = x_top.rearrange("(p i) k -> p i k", i=8)
+        x_rest_v = x_rest.rearrange("(p i) k -> p i k", i=8)
+        zb_v = z_top_bytes.rearrange("(c j t) k -> c j t k", c=NC, t=4)
+        zw_v = z_rest_words.rearrange("g p w -> p g w")
+
+        xt = [alloc(f"xt{h}", [P, RT, A], BF16) for h in range(NH)]
+        xr = [[alloc(f"xr{h}_{b}", [P, 2, B], BF16) for b in range(2)] for h in range(NH)]
+        zb = [alloc(f"zb{c}", [P, 4, A], U8) for c in range(NC)]
+        zw_raw = [alloc(f"zw_raw{c}", [P, 2, 1024], U8) for c in range(NC)]
+        cw = alloc("cw", [P, NC, 2 * R], U8)
+
+        def load_xt(h):
+            nc.sync.dma_start(out=xt[h][:], in_=x_top_v[:, RT * h : RT * (h + 1), :])
+
+        def load_xr(h, b):
+            i = RT * h + 2 * b
+            nc.sync.dma_start(out=xr[h][b][:], in_=x_rest_v[:, i : i + 2, :])
+
+        def load_z(c):
+            nc.sync.dma_start(out=zb[c][:], in_=zb_v[c])
+
+        def load_zw(c):
+            nc.sync.dma_start(out=zw_raw[c][:], in_=zw_v[:, :, 1024 * c : 1024 * (c + 1)])
+
+        load_z(0)
+        load_xt(0)
+        load_zw(0)
+        for q in range(4):
+            nc.sync.dma_start(
+                out=zs_raw[32 * q : 32 * q + 4, :, :].bitcast(I32),
+                in_=z_rest_scales[:, 4 * q : 4 * q + 4, :].rearrange("g q n -> q g n").bitcast(I32),
+            )
+        for q in range(4):
+            nc.sync.dma_start(
+                out=cs[32 * q : 32 * q + 4, :, :].bitcast(I32),
+                in_=alpha_scales[:, 4 * q : 4 * q + 4, :].rearrange("g q n -> q g n").bitcast(I32),
+            )
+        load_xr(0, 0)
+        load_xr(0, 1)
+        load_z(1)
+        load_zw(1)
+        load_xt(1)
+        load_xr(1, 0)
+        load_xr(1, 1)
+        load_z(2)
+        load_zw(2)
+        load_z(3)
+        load_zw(3)
+        nc.sync.dma_start(out=cw[:], in_=alpha_words.rearrange("g p w -> p g w"))
+
+        ident = alloc("ident", [P, P], F32)
+        make_identity(nc, ident[:])
+        one = alloc("one", [P, 1], F32)
+        nc.vector.memset(one[:], 1.0)
+        junk = alloc("junk", [P, 2], F32)
+        nc.scalar.activation(out=junk[:, 0:1], in_=one[:], func=ACT.Ln)
+        gabs = alloc("gabs", [P, NC * 4], F32)
+        gclip = alloc("gclip", [P, NC * 4], F32)
+        gln = alloc("gln", [P, NC * 4], F32)
+        ginv = alloc("ginv", [P, NC * 4], F32)
+        gsign = alloc("gsign", [P, NC * 4], F32)
+        gain2 = gain[:].rearrange("p c t -> p (c t)")
+        nc.scalar.activation(out=gabs[:], in_=gain2, func=ACT.Abs)
+        nc.vector.tensor_scalar(gclip[:], gabs[:], 2.0**-60, 2.0**60, op0=ALU.max, op1=ALU.min)
+        nc.scalar.activation(out=gln[:], in_=gclip[:], func=ACT.Ln)
+        nc.scalar.activation(out=junk[:, 1:2], in_=gln[:, 0:1], func=ACT.Exp)
+        nc.vector.reciprocal(out=ginv[:], in_=gclip[:])
+        nc.vector.tensor_tensor(out=gsign[:], in0=gain2, in1=ginv[:], op=ALU.mult)
+
+        def spread(name, col4):
+            ps = bank("m")
+            ps3 = ps[:].rearrange("p (q a) -> p q a", q=4)
+            for q in range(4):
+                nc.tensor.transpose(ps3[:, q, :], col4[:, q : q + 1].to_broadcast([P, P]), ident[:])
+            row = alloc(name, [P, 512], F32)
+            nc.vector.tensor_copy(out=row[:].rearrange("p (a q) -> p a q", q=4), in_=ps3.rearrange("p q a -> p a q"))
+            return row
+
+        scale_row = spread("scale_row", sc4)
+
+        xq = [[alloc(f"xq{h}_{g}", [P, MH], U32) for g in range(3)] for h in range(NH)]
+        xs = [[alloc(f"xs{h}_{g}", [P, MH], U8) for g in range(3)] for h in range(NH)]
+
+        def turn(dst, col0, sources):
+            ps = bank("m")
+            ps4 = ps[:].rearrange("p (s u r) -> p s u r", s=2, u=2)
+            for s, src in enumerate(sources):
+                words = src.bitcast(F32)
+                for u in range(2):
+                    nc.tensor.transpose(ps4[:, s, u, :], words[:, u : 256 : 2], ident[:])
+            flat = dst[:].rearrange("p m t -> p (m t)").bitcast(F32)
+            nc.scalar.copy(
+                out=flat[:, 2 * col0 : 2 * col0 + 512].rearrange("p (s r u) -> p s r u", s=2, u=2),
+                in_=ps4.rearrange("p s u r -> p s r u"),
+            )
+
+        def x_source(h, g, rt):
+            if g == 0:
+                return xt[h][:, rt, :]
+            return xr[h][rt // 2][:, rt % 2, 512 * (g - 1) : 512 * g]
+
+        def prep_x(h, g):
+            xg = alloc("xg", [P, MH, 4], BF16, bufs=3)
+            for b in range(2):
+                turn(xg, 256 * b, [x_source(h, g, 2 * b), x_source(h, g, 2 * b + 1)])
+            nc.vector.quantize_mx(out=xq[h][g][:].bitcast(FP8X4), scales=xs[h][g][:], in_=xg[:].rearrange("p m t -> p (m t)"))
+
+        zq = [alloc(f"zq{c}", [P, 512], U32) for c in range(NC)]
+        zqs = [alloc(f"zqs{c}", [P, 512], U8) for c in range(NC)]
+        zw = [alloc(f"zw{c}", [P, 2, 1024], U8) for c in range(NC)]
+        zs = [alloc(f"zs{c}", [P, 2, 512], U8) for c in range(NC)]
+        zf = {}
+
+        def z_product(c):
+            zf[c] = alloc("zf", [P, 4, A], BF16, bufs=2)
+            for t in range(4):
+                nc.vector.tensor_tensor(out=zf[c][:, t, :], in0=zb[c][:, t, :].bitcast(FP8), in1=scale_row[:], op=ALU.mult)
+
+        def z_words(c):
+            nc.vector.tensor_copy(
+                out=zs[c][:].rearrange("p g (t j) -> p g t j", t=4),
+                in_=zs_raw[:, :, 512 * c : 512 * (c + 1)].rearrange("p g (j t) -> p g t j", t=4),
+            )
+            for g in range(2):
+                nc.vector.tensor_copy(
+                    out=zw[c][:, g, :].rearrange("p (t j b) -> p t j b", t=4, b=2),
+                    in_=zw_raw[c][:, g, :].rearrange("p (j t b) -> p t j b", t=4, b=2),
+                )
+
+        def z_turn(c):
+            zg = alloc("zg", [P, 512, 4], BF16, bufs=2)
+            for b in range(2):
+                turn(zg, 256 * b, [zf[c][:, 2 * b, :], zf[c][:, 2 * b + 1, :]])
+            nc.vector.quantize_mx(out=zq[c][:].bitcast(FP8X4), scales=zqs[c][:], in_=zg[:].rearrange("p m t -> p (m t)"))
+
+        hq = [[alloc(f"hq{h}_{c}", [P, MH], U32) for c in range(NC)] for h in range(NH)]
+        hqs = [[alloc(f"hqs{h}_{c}", [P, MH], U8) for c in range(NC)] for h in range(NH)]
+
+        def mx_pass(ps, h, c, t, g):
+            if g == 0:
+                lhs = zq[c][:, P * t : P * (t + 1)].bitcast(FP8X4)
+                lhs_scale = zqs[c][:, P * t : P * (t + 1)]
+            else:
+                lhs = zw[c][:, g - 1, 2 * P * t : 2 * P * (t + 1)].bitcast(FP4X4)
+                lhs_scale = zs[c][:, g - 1, P * t : P * (t + 1)]
+            nc.tensor.matmul_mx(
+                out=ps[:], lhsT=lhs, lhsT_scale=lhs_scale,
+                rhs=xq[h][g][:].bitcast(FP8X4), rhs_scale=xs[h][g][:],
+                start=(g == 0), stop=(g == 2),
+            )
+
+        def block(c, h, pass_outer=False):
+            hp = alloc("hp", [P, 4, MH], BF16, bufs=3)
+            hs = alloc("hs", [P, 4, MH], BF16, bufs=3)
+            hg = alloc("hg", [P, MH, 4], BF16, bufs=3)
+            banks = {}
+            if pass_outer:
+                for t in range(4):
+                    banks[t] = bank("u")
+                for g in range(3):
+                    for t in range(4):
+                        mx_pass(banks[t], h, c, t, g)
+            for t in range(4):
+                if not pass_outer:
+                    banks[t] = bank("u")
+                    for g in range(3):
+                        mx_pass(banks[t], h, c, t, g)
+                i = 4 * c + t
+                nc.scalar.activation(out=hp[:, t, :], in_=banks[t][:], func=ACT.Exp, bias=gln[:, i : i + 1])
+                nc.vector.tensor_scalar(hs[:, t, :], hp[:, t, :], gsign[:, i : i + 1], None, op0=ALU.mult)
+            for engine_copy, lo, hi in ((nc.scalar.copy, 0, SPLIT), (nc.vector.tensor_copy, SPLIT, MH)):
+                engine_copy(
+                    out=hg[:, lo:hi, :].rearrange("p (e i) t -> p e t i", i=4),
+                    in_=hs[:, :, lo:hi].rearrange("p t (e i) -> p e t i", i=4),
+                )
+            nc.vector.quantize_mx(out=hq[h][c][:].bitcast(FP8X4), scales=hqs[h][c][:], in_=hg[:].rearrange("p m t -> p (m t)"))
+
+        out_v = out.rearrange("(p i) r -> p i r", i=8)
+
+        def second(h):
+            for rt in range(RT):
+                ps = bank("m")
+                cols = slice(P * rt, P * (rt + 1))
+                for c in range(NC):
+                    nc.tensor.matmul_mx(
+                        out=ps[:], lhsT=hq[h][c][:, cols].bitcast(FP8X4), lhsT_scale=hqs[h][c][:, cols],
+                        rhs=cw[:, c, :].bitcast(FP4X4), rhs_scale=cs[:, c, :],
+                        start=(c == 0), stop=(c == NC - 1),
+                    )
+                i = RT * h + rt
+                res = alloc("res", [P, R], F32, bufs=4)
+                nc.vector.scalar_tensor_tensor(out=res[:], in0=ps[:], scalar=qg[:, i : i + 1], in1=ic_row[:], op0=ALU.mult, op1=ALU.add)
+                nc.sync.dma_start(out=out_v[:, i, :], in_=res[:])
+
+        z_product(0)
+        prep_x(0, 0)
+        z_words(0)
+        z_turn(0)
+        prep_x(0, 1)
+        prep_x(0, 2)
+        block(0, 0, pass_outer=True)
+        z_product(1)
+        for g in range(3):
+            prep_x(1, g)
+        z_words(1)
+        z_turn(1)
+        block(0, 1)
+        ic4f = alloc("ic4f", [P, 4], F32)
+        nc.vector.tensor_copy(out=ic4f[:], in_=ic4[:])
+        ic_row = spread("ic_row", ic4f)
+        z_product(2)
+        block(1, 0)
+        z_words(2)
+        z_turn(2)
+        block(1, 1)
+        z_product(3)
+        block(2, 0)
+        z_words(3)
+        z_turn(3)
+        block(2, 1)
+        block(3, 0)
+        second(0)
+        block(3, 1)
+        second(1)

@@ -22,7 +22,77 @@ NC = L // 512
 NH = 2
 MH = M // NH
 RT = MH // P
-SPLIT = 192
+CUTS = {
+    (0, 0): [(0, 384, 512)],
+    (0, 1): [(0, 256, 512)],
+    (1, 0): [(0, 128, 512)],
+    (1, 1): [(0, 96, 512)],
+    (2, 0): [(0, 32, 512)],
+    (2, 1): [(0, 128, 512)],
+    (3, 0): [(0, 192, 512)],
+    (3, 1): [(0, 32, 256), (256, 320, 512)],
+}
+PASSES = {(c, h): (0, 1, 2) for c in range(4) for h in range(2)}
+EV_VECTOR = set()
+ORDER = [
+    ("gain_clip",), ("load", "xt", 0, 2, 4), ("load", "z", 0), ("gain_ln",), ("spread_t", "scale"), ("spread_v", "scale"),
+    ("prod", 0, 0), ("load", "xt", 0, 0, 2), ("prod", 0, 1), ("load", "xr", 0, 0, 2), ("prod", 0, 2), ("prod", 0, 3),
+    ("tr_x", 0, 0, 0), ("ev_x", 0, 0, 0), ("load", "xr", 0, 2, 4), ("tr_x", 0, 0, 1), ("tr_x", 0, 1, 0), ("load", "xt", 1, 0, 4),
+    ("load", "xr", 1, 0, 4), ("ev_x", 0, 0, 1), ("gain_sign",), ("tr_z", 0, 0), ("ln_table",), ("load", "zw", 0),
+    ("tr_z", 0, 1), ("ev_x", 0, 1, 0), ("q_x", 0, 0), ("tr_x", 0, 1, 1), ("ev_z", 0, 0), ("ev_z", 0, 1),
+    ("tr_x", 0, 2, 0), ("tr_x", 0, 2, 1), ("ev_x", 0, 1, 1), ("ev_x", 0, 2, 0), ("tr_x", 1, 0, 0), ("load", "zs"),
+    ("ev_x", 1, 0, 0), ("load", "z", 1), ("q_z", 0), ("tr_x", 1, 0, 1), ("q_x", 0, 1), ("mx", 0, 0, 0, 0),
+    ("mx", 0, 0, 1, 0), ("ev_x", 0, 2, 1), ("ev_x", 1, 0, 1), ("perm_w", 0, 0), ("mx", 0, 0, 2, 0), ("q_x", 0, 2),
+    ("tr_x", 1, 1, 0), ("ic_cast",), ("tr_x", 1, 1, 1), ("mx", 0, 0, 3, 0), ("perm_s", 0), ("prod", 1, 0),
+    ("mx", 0, 0, 0, 1), ("exp_table",), ("prod", 1, 1), ("ev_x", 1, 1, 0), ("mx", 0, 0, 1, 1), ("ev_x", 1, 1, 1),
+    ("tr_x", 1, 2, 0), ("perm_w", 0, 1), ("prod", 1, 2), ("tr_z", 1, 0), ("load", "z", 2), ("mx", 0, 0, 2, 1),
+    ("mx", 0, 0, 3, 1), ("mx", 0, 0, 0, 2), ("mx", 0, 0, 1, 2), ("prod", 1, 3), ("q_x", 1, 0), ("load", "zw", 1),
+    ("mx", 0, 0, 2, 2), ("perm_s", 1), ("mx", 0, 0, 3, 2), ("prod", 2, 0), ("prod", 2, 1), ("ev_x", 1, 2, 0),
+    ("q_x", 1, 1), ("exp", 0, 0, 0, 0), ("tr_x", 1, 2, 1), ("ev_z", 1, 0), ("sign", 0, 0, 0, 0), ("ev_x", 1, 2, 1),
+    ("tr_z", 1, 1), ("spread_t", "ic"), ("exp", 0, 0, 1, 0), ("q_x", 1, 2), ("ev_z", 1, 1), ("tr_z", 2, 0),
+    ("mx", 0, 1, 0, 0), ("mx", 0, 1, 0, 1), ("mx", 0, 1, 0, 2), ("exp", 0, 0, 2, 0), ("sign", 0, 0, 1, 0), ("perm_w", 1, 0),
+    ("exp", 0, 0, 3, 0), ("mx", 0, 1, 1, 0), ("q_z", 1), ("mx", 0, 1, 1, 1), ("mx", 0, 1, 1, 2), ("perm_w", 1, 1),
+    ("sign", 0, 0, 2, 0), ("mx", 0, 1, 2, 0), ("ev_z", 2, 0), ("exp", 0, 1, 0, 0), ("prod", 2, 2), ("prod", 2, 3),
+    ("mx", 0, 1, 2, 1), ("mx", 0, 1, 2, 2), ("exp", 0, 1, 1, 0), ("mx", 0, 1, 3, 0), ("mx", 0, 1, 3, 1), ("load", "zw", 2),
+    ("load", "zw", 3), ("mx", 0, 1, 3, 2), ("mx", 1, 0, 0, 0), ("exp", 0, 1, 2, 0), ("mx", 1, 0, 0, 1), ("load", "z", 3),
+    ("mx", 1, 0, 0, 2), ("sign", 0, 0, 3, 0), ("mx", 1, 0, 1, 0), ("exp", 0, 1, 3, 0), ("mx", 1, 0, 1, 1), ("sign", 0, 1, 0, 0),
+    ("mx", 1, 0, 1, 2), ("prod", 3, 0), ("perm_s", 2), ("prod", 3, 1), ("mx", 1, 0, 2, 0), ("sign", 0, 1, 1, 0),
+    ("sign", 0, 1, 2, 0), ("spread_v", "ic"), ("mx", 1, 0, 2, 1), ("mx", 1, 0, 2, 2), ("exp", 1, 0, 0, 0), ("mx", 1, 0, 3, 0),
+    ("tr_z", 2, 1), ("tr_z", 3, 0), ("perm_w", 2, 0), ("il_v", 0, 0, 0), ("mx", 1, 0, 3, 1), ("il_s", 0, 0, 0),
+    ("mx", 1, 0, 3, 2), ("sign", 0, 1, 3, 0), ("mx", 1, 1, 0, 0), ("exp", 1, 0, 1, 0), ("exp", 1, 0, 2, 0), ("mx", 1, 1, 0, 1),
+    ("mx", 1, 1, 0, 2), ("mx", 1, 1, 1, 0), ("sign", 1, 0, 0, 0), ("mx", 1, 1, 1, 1), ("perm_w", 2, 1), ("mx", 1, 1, 1, 2),
+    ("ev_z", 2, 1), ("perm_w", 3, 0), ("mx", 1, 1, 2, 0), ("sign", 1, 0, 1, 0), ("il_v", 0, 1, 0), ("mx", 1, 1, 2, 1),
+    ("perm_w", 3, 1), ("ev_z", 3, 0), ("load", "cs"), ("mx", 1, 1, 2, 2), ("exp", 1, 0, 3, 0), ("exp", 1, 1, 0, 0),
+    ("exp", 1, 1, 1, 0), ("q_z", 2), ("q_h", 0, 0, 0), ("sign", 1, 0, 2, 0), ("mx", 1, 1, 3, 0), ("prod", 3, 2),
+    ("mx", 1, 1, 3, 1), ("perm_s", 3), ("mx", 1, 1, 3, 2), ("mx", 2, 0, 0, 0), ("exp", 1, 1, 2, 0), ("sign", 1, 0, 3, 0),
+    ("mx", 2, 0, 0, 1), ("exp", 1, 1, 3, 0), ("mx", 2, 0, 0, 2), ("mx", 2, 0, 1, 0), ("exp", 2, 0, 0, 0), ("sign", 1, 1, 0, 0),
+    ("mx", 2, 0, 1, 1), ("mx", 2, 0, 1, 2), ("prod", 3, 3), ("il_s", 0, 1, 0), ("sign", 1, 1, 1, 0), ("il_v", 1, 0, 0),
+    ("sign", 1, 1, 2, 0), ("mx", 2, 0, 2, 0), ("mx", 2, 0, 2, 1), ("mx", 2, 0, 2, 2), ("mx", 2, 0, 3, 0), ("mx", 2, 0, 3, 1),
+    ("q_h", 0, 1, 0), ("mx", 2, 0, 3, 2), ("tr_z", 3, 1), ("sign", 1, 1, 3, 0), ("mx", 2, 1, 0, 0), ("il_s", 1, 0, 0),
+    ("exp", 2, 0, 1, 0), ("sign", 2, 0, 0, 0), ("mx", 2, 1, 0, 1), ("mx", 2, 1, 0, 2), ("mx", 2, 1, 1, 0), ("sign", 2, 0, 1, 0),
+    ("load", "cw"), ("mx", 2, 1, 1, 1), ("q_h", 1, 0, 0), ("exp", 2, 0, 2, 0), ("exp", 2, 0, 3, 0), ("mx", 2, 1, 1, 2),
+    ("ev_z", 3, 1), ("exp", 2, 1, 0, 0), ("sign", 2, 0, 2, 0), ("mx", 2, 1, 2, 0), ("mx", 2, 1, 2, 1), ("q_z", 3),
+    ("mx", 2, 1, 2, 2), ("exp", 2, 1, 1, 0), ("sign", 2, 0, 3, 0), ("mx", 2, 1, 3, 0), ("exp", 2, 1, 2, 0), ("sign", 2, 1, 0, 0),
+    ("il_v", 1, 1, 0), ("mx", 2, 1, 3, 1), ("il_v", 2, 0, 0), ("sign", 2, 1, 1, 0), ("mx", 2, 1, 3, 2), ("sign", 2, 1, 2, 0),
+    ("mx", 3, 0, 0, 0), ("il_s", 1, 1, 0), ("mx", 3, 0, 0, 1), ("mx", 3, 0, 0, 2), ("exp", 2, 1, 3, 0), ("sign", 2, 1, 3, 0),
+    ("mx", 3, 0, 1, 0), ("q_h", 1, 1, 0), ("exp", 3, 0, 0, 0), ("mx", 3, 0, 1, 1), ("mx", 3, 0, 1, 2), ("exp", 3, 0, 1, 0),
+    ("mx", 3, 0, 2, 0), ("sign", 3, 0, 0, 0), ("mx", 3, 0, 2, 1), ("mx", 3, 0, 2, 2), ("mx", 3, 0, 3, 0), ("mx", 3, 0, 3, 1),
+    ("mx", 3, 0, 3, 2), ("il_s", 2, 0, 0), ("sign", 3, 0, 1, 0), ("exp", 3, 0, 2, 0), ("mx", 3, 1, 0, 0), ("q_h", 2, 0, 0),
+    ("exp", 3, 0, 3, 0), ("mx", 3, 1, 0, 1), ("mx2", 0, 0, 0), ("mx", 3, 1, 0, 2), ("mx2", 0, 0, 1), ("il_s", 2, 1, 0),
+    ("sign", 3, 0, 2, 0), ("mx", 3, 1, 1, 0), ("il_v", 2, 1, 0), ("mx", 3, 1, 1, 1), ("exp", 3, 1, 0, 0), ("mx", 3, 1, 1, 2),
+    ("sign", 3, 0, 3, 0), ("il_v", 3, 0, 0), ("mx2", 0, 0, 2), ("il_s", 3, 0, 0), ("mx", 3, 1, 2, 0), ("sign", 3, 1, 0, 0),
+    ("exp", 3, 1, 0, 1), ("mx", 3, 1, 2, 1), ("mx", 3, 1, 2, 2), ("q_h", 3, 0, 0), ("exp", 3, 1, 1, 0), ("mx", 3, 1, 3, 0),
+    ("sign", 3, 1, 0, 1), ("mx", 3, 1, 3, 1), ("exp", 3, 1, 1, 1), ("sign", 3, 1, 1, 0), ("mx2", 0, 0, 3), ("sign", 3, 1, 1, 1),
+    ("mx", 3, 1, 3, 2), ("exp", 3, 1, 2, 0), ("sign", 3, 1, 2, 0), ("exp", 3, 1, 2, 1), ("mx2", 0, 1, 0), ("finish", 0, 0),
+    ("q_h", 2, 1, 0), ("mx2", 0, 1, 1), ("mx2", 0, 1, 2), ("exp", 3, 1, 3, 0), ("sign", 3, 1, 2, 1), ("mx2", 0, 1, 3),
+    ("sign", 3, 1, 3, 0), ("mx2", 0, 2, 0), ("mx2", 0, 2, 1), ("mx2", 0, 2, 2), ("exp", 3, 1, 3, 1), ("mx2", 0, 2, 3),
+    ("il_s", 3, 1, 0), ("mx2", 0, 3, 0), ("mx2", 0, 3, 1), ("finish", 0, 1), ("il_v", 3, 1, 0), ("finish", 0, 2),
+    ("sign", 3, 1, 3, 1), ("mx2", 0, 3, 2), ("mx2", 0, 3, 3), ("mx2", 1, 3, 0), ("mx2", 1, 0, 0), ("il_s", 3, 1, 1),
+    ("mx2", 1, 2, 0), ("finish", 0, 3), ("mx2", 1, 0, 1), ("mx2", 1, 3, 1), ("il_v", 3, 1, 1), ("mx2", 1, 1, 0),
+    ("q_h", 3, 1, 0), ("mx2", 1, 0, 2), ("mx2", 1, 1, 1), ("q_h", 3, 1, 1), ("mx2", 1, 0, 3), ("finish", 1, 0),
+    ("mx2", 1, 1, 2), ("mx2", 1, 1, 3), ("finish", 1, 1), ("mx2", 1, 2, 1), ("mx2", 1, 2, 2), ("mx2", 1, 2, 3),
+    ("mx2", 1, 3, 2), ("mx2", 1, 3, 3), ("finish", 1, 2), ("finish", 1, 3),
+]
 
 
 def tile_landmark_kernel_ridge_s3_kernel(
@@ -40,6 +110,8 @@ def tile_landmark_kernel_ridge_s3_kernel(
         def bank(name):
             return psum.tile([P, 512], F32, name=name)
 
+        ctx.enter_context(tc.manual_schedule())
+
         sc4 = alloc("sc4", [P, 4], F32)
         gain = alloc("gain", [P, NC, 4], BF16)
         qg = alloc("qg", [P, 8], BF16)
@@ -48,6 +120,10 @@ def tile_landmark_kernel_ridge_s3_kernel(
         nc.scalar.dma_start(out=gain[:], in_=landmark_gain.rearrange("(c j t) -> j c t", c=NC, t=4))
         nc.gpsimd.dma_start(out=qg[:], in_=query_gain.rearrange("(p i) -> p i", i=8))
         nc.gpsimd.dma_start(out=ic4[:], in_=intercept.rearrange("(p q) -> p q", q=4))
+        ident = alloc("ident", [P, P], F32)
+        make_identity(nc, ident[:])
+        one = alloc("one", [P, 1], F32)
+        nc.vector.memset(one[:], 1.0)
 
         zs_raw = alloc("zs_raw", [P, 2, L], U8)
         cs = alloc("cs", [P, NC, R], U8)
@@ -60,17 +136,10 @@ def tile_landmark_kernel_ridge_s3_kernel(
         zw_v = z_rest_words.rearrange("g p w -> p g w")
 
         xt = [alloc(f"xt{h}", [P, RT, A], BF16) for h in range(NH)]
-        xr = [[alloc(f"xr{h}_{b}", [P, 2, B], BF16) for b in range(2)] for h in range(NH)]
+        xr = [alloc(f"xr{h}", [P, RT, B], BF16) for h in range(NH)]
         zb = [alloc(f"zb{c}", [P, 4, A], U8) for c in range(NC)]
         zw_raw = [alloc(f"zw_raw{c}", [P, 2, 1024], U8) for c in range(NC)]
         cw = alloc("cw", [P, NC, 2 * R], U8)
-
-        def load_xt(h):
-            nc.sync.dma_start(out=xt[h][:], in_=x_top_v[:, RT * h : RT * (h + 1), :])
-
-        def load_xr(h, b):
-            i = RT * h + 2 * b
-            nc.sync.dma_start(out=xr[h][b][:], in_=x_rest_v[:, i : i + 2, :])
 
         def load_z(c):
             nc.sync.dma_start(out=zb[c][:], in_=zb_v[c])
@@ -78,88 +147,104 @@ def tile_landmark_kernel_ridge_s3_kernel(
         def load_zw(c):
             nc.sync.dma_start(out=zw_raw[c][:], in_=zw_v[:, :, 1024 * c : 1024 * (c + 1)])
 
-        load_z(0)
-        load_xt(0)
-        load_zw(0)
-        for q in range(4):
-            nc.sync.dma_start(
-                out=zs_raw[32 * q : 32 * q + 4, :, :].bitcast(I32),
-                in_=z_rest_scales[:, 4 * q : 4 * q + 4, :].rearrange("g q n -> q g n").bitcast(I32),
-            )
-        for q in range(4):
-            nc.sync.dma_start(
-                out=cs[32 * q : 32 * q + 4, :, :].bitcast(I32),
-                in_=alpha_scales[:, 4 * q : 4 * q + 4, :].rearrange("g q n -> q g n").bitcast(I32),
-            )
-        load_xr(0, 0)
-        load_xr(0, 1)
-        load_z(1)
-        load_zw(1)
-        load_xt(1)
-        load_xr(1, 0)
-        load_xr(1, 1)
-        load_z(2)
-        load_zw(2)
-        load_z(3)
-        load_zw(3)
-        nc.sync.dma_start(out=cw[:], in_=alpha_words.rearrange("g p w -> p g w"))
+        def load_x(dst, src, h, lo=0, hi=RT):
+            nc.sync.dma_start(out=dst[h][:, lo:hi, :], in_=src[:, RT * h + lo : RT * h + hi, :])
 
-        ident = alloc("ident", [P, P], F32)
-        make_identity(nc, ident[:])
-        one = alloc("one", [P, 1], F32)
-        nc.vector.memset(one[:], 1.0)
+        def load_scales(dst, src):
+            for q in range(4):
+                nc.sync.dma_start(
+                    out=dst[32 * q : 32 * q + 4, :, :].bitcast(I32),
+                    in_=src[:, 4 * q : 4 * q + 4, :].rearrange("g q n -> q g n").bitcast(I32),
+                )
+
+        def load(what, *args):
+            if what == "z":
+                load_z(*args)
+            elif what == "zw":
+                load_zw(*args)
+            elif what == "xt":
+                load_x(xt, x_top_v, *args)
+            elif what == "xr":
+                load_x(xr, x_rest_v, *args)
+            elif what == "zs":
+                load_scales(zs_raw, z_rest_scales)
+            elif what == "cs":
+                load_scales(cs, alpha_scales)
+            else:
+                nc.sync.dma_start(out=cw[:], in_=alpha_words.rearrange("g p w -> p g w"))
+
+        banks = {}
+        grouped = {}
         junk = alloc("junk", [P, 2], F32)
-        nc.scalar.activation(out=junk[:, 0:1], in_=one[:], func=ACT.Ln)
         gabs = alloc("gabs", [P, NC * 4], F32)
         gclip = alloc("gclip", [P, NC * 4], F32)
         gln = alloc("gln", [P, NC * 4], F32)
         ginv = alloc("ginv", [P, NC * 4], F32)
         gsign = alloc("gsign", [P, NC * 4], F32)
         gain2 = gain[:].rearrange("p c t -> p (c t)")
-        nc.scalar.activation(out=gabs[:], in_=gain2, func=ACT.Abs)
-        nc.vector.tensor_scalar(gclip[:], gabs[:], 2.0**-60, 2.0**60, op0=ALU.max, op1=ALU.min)
-        nc.scalar.activation(out=gln[:], in_=gclip[:], func=ACT.Ln)
-        nc.scalar.activation(out=junk[:, 1:2], in_=gln[:, 0:1], func=ACT.Exp)
-        nc.vector.reciprocal(out=ginv[:], in_=gclip[:])
-        nc.vector.tensor_tensor(out=gsign[:], in0=gain2, in1=ginv[:], op=ALU.mult)
+        def ln_table():
+            nc.scalar.activation(out=junk[:, 0:1], in_=one[:], func=ACT.Ln)
 
-        def spread(name, col4):
+        def gain_clip():
+            nc.vector.scalar_tensor_tensor(out=gabs[:], in0=gain2, scalar=-1.0, in1=gain2, op0=ALU.mult, op1=ALU.max)
+            nc.vector.tensor_scalar(gclip[:], gabs[:], 2.0**-60, 2.0**60, op0=ALU.max, op1=ALU.min)
+
+        def gain_ln():
+            nc.scalar.activation(out=gln[:], in_=gclip[:], func=ACT.Ln)
+
+        scale_row = alloc("scale_row", [P, 512], F32)
+        ic_row = alloc("ic_row", [P, R], F32)
+        ic4f = alloc("ic4f", [P, 4], F32)
+
+        def ic_cast():
+            nc.vector.tensor_copy(out=ic4f[:], in_=ic4[:])
+
+        def spread_t(which):
+            col4 = sc4 if which == "scale" else ic4f
             ps = bank("m")
             ps3 = ps[:].rearrange("p (q a) -> p q a", q=4)
             for q in range(4):
                 nc.tensor.transpose(ps3[:, q, :], col4[:, q : q + 1].to_broadcast([P, P]), ident[:])
-            row = alloc(name, [P, 512], F32)
-            nc.vector.tensor_copy(out=row[:].rearrange("p (a q) -> p a q", q=4), in_=ps3.rearrange("p q a -> p a q"))
-            return row
+            banks[which] = ps3
 
-        scale_row = spread("scale_row", sc4)
+        def spread_v(which):
+            row = scale_row if which == "scale" else ic_row
+            nc.vector.tensor_copy(out=row[:].rearrange("p (a q) -> p a q", q=4), in_=banks[which].rearrange("p q a -> p a q"))
 
         xq = [[alloc(f"xq{h}_{g}", [P, MH], U32) for g in range(3)] for h in range(NH)]
         xs = [[alloc(f"xs{h}_{g}", [P, MH], U8) for g in range(3)] for h in range(NH)]
-
-        def turn(dst, col0, sources):
+        def turn(key, sources):
             ps = bank("m")
             ps4 = ps[:].rearrange("p (s u r) -> p s u r", s=2, u=2)
             for s, src in enumerate(sources):
                 words = src.bitcast(F32)
                 for u in range(2):
                     nc.tensor.transpose(ps4[:, s, u, :], words[:, u : 256 : 2], ident[:])
+            banks[key] = ps4
+
+        def emit_out(key, dst, half, engine_copy):
             flat = dst[:].rearrange("p m t -> p (m t)").bitcast(F32)
-            nc.scalar.copy(
-                out=flat[:, 2 * col0 : 2 * col0 + 512].rearrange("p (s r u) -> p s r u", s=2, u=2),
-                in_=ps4.rearrange("p s u r -> p s r u"),
+            engine_copy(
+                out=flat[:, 512 * half : 512 * half + 512].rearrange("p (s r u) -> p s r u", s=2, u=2),
+                in_=banks[key].rearrange("p s u r -> p s r u"),
             )
 
         def x_source(h, g, rt):
             if g == 0:
                 return xt[h][:, rt, :]
-            return xr[h][rt // 2][:, rt % 2, 512 * (g - 1) : 512 * g]
+            return xr[h][:, rt, 512 * (g - 1) : 512 * g]
 
-        def prep_x(h, g):
-            xg = alloc("xg", [P, MH, 4], BF16, bufs=3)
-            for b in range(2):
-                turn(xg, 256 * b, [x_source(h, g, 2 * b), x_source(h, g, 2 * b + 1)])
-            nc.vector.quantize_mx(out=xq[h][g][:].bitcast(FP8X4), scales=xs[h][g][:], in_=xg[:].rearrange("p m t -> p (m t)"))
+        def tr_x(h, g, b):
+            turn(("x", h, g, b), [x_source(h, g, 2 * b), x_source(h, g, 2 * b + 1)])
+
+        def ev_x(h, g, b):
+            engine_copy = nc.vector.tensor_copy if ("x", h, g, b) in EV_VECTOR else nc.scalar.copy
+            if ("x", h, g) not in grouped:
+                grouped["x", h, g] = alloc("xg", [P, MH, 4], BF16, bufs=4)
+            emit_out(("x", h, g, b), grouped["x", h, g], b, engine_copy)
+
+        def q_x(h, g):
+            nc.vector.quantize_mx(out=xq[h][g][:].bitcast(FP8X4), scales=xs[h][g][:], in_=grouped["x", h, g][:].rearrange("p m t -> p (m t)"))
 
         zq = [alloc(f"zq{c}", [P, 512], U32) for c in range(NC)]
         zqs = [alloc(f"zqs{c}", [P, 512], U8) for c in range(NC)]
@@ -167,32 +252,43 @@ def tile_landmark_kernel_ridge_s3_kernel(
         zs = [alloc(f"zs{c}", [P, 2, 512], U8) for c in range(NC)]
         zf = {}
 
-        def z_product(c):
-            zf[c] = alloc("zf", [P, 4, A], BF16, bufs=2)
-            for t in range(4):
-                nc.vector.tensor_tensor(out=zf[c][:, t, :], in0=zb[c][:, t, :].bitcast(FP8), in1=scale_row[:], op=ALU.mult)
+        def prod(c, t):
+            if c not in zf:
+                zf[c] = alloc("zf", [P, 4, A], BF16, bufs=3)
+            nc.vector.tensor_tensor(out=zf[c][:, t, :], in0=zb[c][:, t, :].bitcast(FP8), in1=scale_row[:], op=ALU.mult)
 
-        def z_words(c):
+        def perm_s(c):
             nc.vector.tensor_copy(
                 out=zs[c][:].rearrange("p g (t j) -> p g t j", t=4),
                 in_=zs_raw[:, :, 512 * c : 512 * (c + 1)].rearrange("p g (j t) -> p g t j", t=4),
             )
-            for g in range(2):
-                nc.vector.tensor_copy(
-                    out=zw[c][:, g, :].rearrange("p (t j b) -> p t j b", t=4, b=2),
-                    in_=zw_raw[c][:, g, :].rearrange("p (j t b) -> p t j b", t=4, b=2),
-                )
 
-        def z_turn(c):
-            zg = alloc("zg", [P, 512, 4], BF16, bufs=2)
-            for b in range(2):
-                turn(zg, 256 * b, [zf[c][:, 2 * b, :], zf[c][:, 2 * b + 1, :]])
-            nc.vector.quantize_mx(out=zq[c][:].bitcast(FP8X4), scales=zqs[c][:], in_=zg[:].rearrange("p m t -> p (m t)"))
+        def perm_w(c, g):
+            nc.vector.tensor_copy(
+                out=zw[c][:, g, :].rearrange("p (t j b) -> p t j b", t=4, b=2),
+                in_=zw_raw[c][:, g, :].rearrange("p (j t b) -> p t j b", t=4, b=2),
+            )
+
+        def tr_z(c, b):
+            turn(("z", c, b), [zf[c][:, 2 * b, :], zf[c][:, 2 * b + 1, :]])
+
+        def ev_z(c, b):
+            engine_copy = nc.vector.tensor_copy if ("z", c, b) in EV_VECTOR else nc.scalar.copy
+            if ("z", c) not in grouped:
+                grouped["z", c] = alloc("zg", [P, 512, 4], BF16, bufs=3)
+            emit_out(("z", c, b), grouped["z", c], b, engine_copy)
+
+        def q_z(c):
+            nc.vector.quantize_mx(out=zq[c][:].bitcast(FP8X4), scales=zqs[c][:], in_=grouped["z", c][:].rearrange("p m t -> p (m t)"))
 
         hq = [[alloc(f"hq{h}_{c}", [P, MH], U32) for c in range(NC)] for h in range(NH)]
         hqs = [[alloc(f"hqs{h}_{c}", [P, MH], U8) for c in range(NC)] for h in range(NH)]
+        planes = {}
 
-        def mx_pass(ps, h, c, t, g):
+        def mx(c, h, t, g):
+            order = PASSES[c, h]
+            if g == order[0]:
+                banks["u", c, h, t] = bank("u")
             if g == 0:
                 lhs = zq[c][:, P * t : P * (t + 1)].bitcast(FP8X4)
                 lhs_scale = zqs[c][:, P * t : P * (t + 1)]
@@ -200,81 +296,73 @@ def tile_landmark_kernel_ridge_s3_kernel(
                 lhs = zw[c][:, g - 1, 2 * P * t : 2 * P * (t + 1)].bitcast(FP4X4)
                 lhs_scale = zs[c][:, g - 1, P * t : P * (t + 1)]
             nc.tensor.matmul_mx(
-                out=ps[:], lhsT=lhs, lhsT_scale=lhs_scale,
+                out=banks["u", c, h, t][:], lhsT=lhs, lhsT_scale=lhs_scale,
                 rhs=xq[h][g][:].bitcast(FP8X4), rhs_scale=xs[h][g][:],
-                start=(g == 0), stop=(g == 2),
+                start=(g == order[0]), stop=(g == order[2]),
             )
 
-        def block(c, h, pass_outer=False):
-            hp = alloc("hp", [P, 4, MH], BF16, bufs=3)
-            hs = alloc("hs", [P, 4, MH], BF16, bufs=3)
-            hg = alloc("hg", [P, MH, 4], BF16, bufs=3)
-            banks = {}
-            if pass_outer:
-                for t in range(4):
-                    banks[t] = bank("u")
-                for g in range(3):
-                    for t in range(4):
-                        mx_pass(banks[t], h, c, t, g)
-            for t in range(4):
-                if not pass_outer:
-                    banks[t] = bank("u")
-                    for g in range(3):
-                        mx_pass(banks[t], h, c, t, g)
-                i = 4 * c + t
-                nc.scalar.activation(out=hp[:, t, :], in_=banks[t][:], func=ACT.Exp, bias=gln[:, i : i + 1])
-                nc.vector.tensor_scalar(hs[:, t, :], hp[:, t, :], gsign[:, i : i + 1], None, op0=ALU.mult)
-            for engine_copy, lo, hi in ((nc.scalar.copy, 0, SPLIT), (nc.vector.tensor_copy, SPLIT, MH)):
-                engine_copy(
-                    out=hg[:, lo:hi, :].rearrange("p (e i) t -> p e t i", i=4),
-                    in_=hs[:, :, lo:hi].rearrange("p t (e i) -> p e t i", i=4),
-                )
-            nc.vector.quantize_mx(out=hq[h][c][:].bitcast(FP8X4), scales=hqs[h][c][:], in_=hg[:].rearrange("p m t -> p (m t)"))
+        def exp(c, h, t, part=0):
+            lo, cut, hi = CUTS[c, h][part]
+            if ("hp", c, h) not in planes:
+                planes["hp", c, h] = alloc("hp", [P, 4, MH], BF16, bufs=3)
+                planes["hs", c, h] = alloc("hs", [P, 4, MH], BF16, bufs=3)
+                planes["hg", c, h] = alloc("hg", [P, MH, 4], BF16, bufs=3)
+            i = 4 * c + t
+            nc.scalar.activation(out=planes["hp", c, h][:, t, lo:hi], in_=banks["u", c, h, t][:, lo:hi], func=ACT.Exp, bias=gln[:, i : i + 1])
+
+        def sign(c, h, t, part=0):
+            lo, cut, hi = CUTS[c, h][part]
+            i = 4 * c + t
+            nc.vector.tensor_scalar(planes["hs", c, h][:, t, lo:hi], planes["hp", c, h][:, t, lo:hi], gsign[:, i : i + 1], None, op0=ALU.mult)
+
+        def il(c, h, engine_copy, lo, hi):
+            engine_copy(
+                out=planes["hg", c, h][:, lo:hi, :].rearrange("p (e i) t -> p e t i", i=4),
+                in_=planes["hs", c, h][:, :, lo:hi].rearrange("p t (e i) -> p e t i", i=4),
+            )
+
+        def il_s(c, h, part=0):
+            lo, cut, hi = CUTS[c, h][part]
+            il(c, h, nc.scalar.copy, lo, cut)
+
+        def il_v(c, h, part=0):
+            lo, cut, hi = CUTS[c, h][part]
+            il(c, h, nc.vector.tensor_copy, cut, hi)
+
+        def q_h(c, h, part=0):
+            lo, cut, hi = CUTS[c, h][part]
+            nc.vector.quantize_mx(
+                out=hq[h][c][:, lo:hi].bitcast(FP8X4), scales=hqs[h][c][:, lo:hi],
+                in_=planes["hg", c, h][:, lo:hi, :].rearrange("p m t -> p (m t)"),
+            )
 
         out_v = out.rearrange("(p i) r -> p i r", i=8)
 
-        def second(h):
-            for rt in range(RT):
-                ps = bank("m")
-                cols = slice(P * rt, P * (rt + 1))
-                for c in range(NC):
-                    nc.tensor.matmul_mx(
-                        out=ps[:], lhsT=hq[h][c][:, cols].bitcast(FP8X4), lhsT_scale=hqs[h][c][:, cols],
-                        rhs=cw[:, c, :].bitcast(FP4X4), rhs_scale=cs[:, c, :],
-                        start=(c == 0), stop=(c == NC - 1),
-                    )
-                i = RT * h + rt
-                res = alloc("res", [P, R], F32, bufs=4)
-                nc.vector.scalar_tensor_tensor(out=res[:], in0=ps[:], scalar=qg[:, i : i + 1], in1=ic_row[:], op0=ALU.mult, op1=ALU.add)
-                nc.sync.dma_start(out=out_v[:, i, :], in_=res[:])
+        def mx2(h, rt, c):
+            if c == 0:
+                banks["o", h, rt] = bank("m")
+            cols = slice(P * rt, P * (rt + 1))
+            nc.tensor.matmul_mx(
+                out=banks["o", h, rt][:], lhsT=hq[h][c][:, cols].bitcast(FP8X4), lhsT_scale=hqs[h][c][:, cols],
+                rhs=cw[:, c, :].bitcast(FP4X4), rhs_scale=cs[:, c, :],
+                start=(c == 0), stop=(c == NC - 1),
+            )
 
-        z_product(0)
-        prep_x(0, 0)
-        z_words(0)
-        z_turn(0)
-        prep_x(0, 1)
-        prep_x(0, 2)
-        block(0, 0, pass_outer=True)
-        z_product(1)
-        for g in range(3):
-            prep_x(1, g)
-        z_words(1)
-        z_turn(1)
-        block(0, 1)
-        ic4f = alloc("ic4f", [P, 4], F32)
-        nc.vector.tensor_copy(out=ic4f[:], in_=ic4[:])
-        ic_row = spread("ic_row", ic4f)
-        z_product(2)
-        block(1, 0)
-        z_words(2)
-        z_turn(2)
-        block(1, 1)
-        z_product(3)
-        block(2, 0)
-        z_words(3)
-        z_turn(3)
-        block(2, 1)
-        block(3, 0)
-        second(0)
-        block(3, 1)
-        second(1)
+        def finish(h, rt):
+            i = RT * h + rt
+            res = alloc("res", [P, R], F32, bufs=4)
+            nc.vector.scalar_tensor_tensor(out=res[:], in0=banks["o", h, rt][:], scalar=qg[:, i : i + 1], in1=ic_row[:], op0=ALU.mult, op1=ALU.add)
+            nc.sync.dma_start(out=out_v[:, i, :], in_=res[:])
+
+        def gain_sign():
+            nc.vector.reciprocal(out=ginv[:], in_=gclip[:])
+            nc.vector.tensor_tensor(out=gsign[:], in0=gain2, in1=ginv[:], op=ALU.mult)
+
+        def exp_table():
+            nc.scalar.activation(out=junk[:, 1:2], in_=gln[:, 0:1], func=ACT.Exp)
+
+        jobs = dict(load=load, ic_cast=ic_cast, ln_table=ln_table, gain_clip=gain_clip, gain_ln=gain_ln, gain_sign=gain_sign, exp_table=exp_table, spread_t=spread_t, spread_v=spread_v,
+                    tr_x=tr_x, ev_x=ev_x, q_x=q_x, prod=prod, perm_s=perm_s, perm_w=perm_w, tr_z=tr_z, ev_z=ev_z, q_z=q_z, mx=mx, exp=exp, sign=sign,
+                    il_s=il_s, il_v=il_v, q_h=q_h, mx2=mx2, finish=finish)
+        for name, *args in ORDER:
+            jobs[name](*args)

from contextlib import ExitStack

import concourse.mybir as mybir
from concourse.masks import make_identity

M, A, B, L, R = 1024, 512, 1024, 2048, 512
FLOPS = 2 * M * (A + B) * L + 2 * M * L * R

F32 = mybir.dt.float32
BF16 = mybir.dt.bfloat16
U32 = mybir.dt.uint32
I32 = mybir.dt.int32
U8 = mybir.dt.uint8
FP8 = mybir.dt.float8_e4m3fn
FP8X4 = mybir.dt.float8_e4m3fn_x4
FP4X4 = mybir.dt.float4_e2m1fn_x4
ALU = mybir.AluOpType
ACT = mybir.ActivationFunctionType

P = 128
NC = L // 512
NH = 2
MH = M // NH
RT = MH // P
CUTS = {
    (0, 0): [(0, 384, 512)],
    (0, 1): [(0, 256, 512)],
    (1, 0): [(0, 128, 512)],
    (1, 1): [(0, 96, 512)],
    (2, 0): [(0, 32, 512)],
    (2, 1): [(0, 128, 512)],
    (3, 0): [(0, 192, 512)],
    (3, 1): [(0, 32, 256), (256, 320, 512)],
}
PASSES = {(c, h): (0, 1, 2) for c in range(4) for h in range(2)}
EV_VECTOR = set()
ORDER = [
    ("gain_clip",), ("load", "xt", 0, 2, 4), ("load", "z", 0), ("gain_ln",), ("spread_t", "scale"), ("spread_v", "scale"),
    ("prod", 0, 0), ("load", "xt", 0, 0, 2), ("prod", 0, 1), ("load", "xr", 0, 0, 2), ("prod", 0, 2), ("prod", 0, 3),
    ("tr_x", 0, 0, 0), ("ev_x", 0, 0, 0), ("load", "xr", 0, 2, 4), ("tr_x", 0, 0, 1), ("tr_x", 0, 1, 0), ("load", "xt", 1, 0, 4),
    ("load", "xr", 1, 0, 4), ("ev_x", 0, 0, 1), ("gain_sign",), ("tr_z", 0, 0), ("ln_table",), ("load", "zw", 0),
    ("tr_z", 0, 1), ("ev_x", 0, 1, 0), ("q_x", 0, 0), ("tr_x", 0, 1, 1), ("ev_z", 0, 0), ("ev_z", 0, 1),
    ("tr_x", 0, 2, 0), ("tr_x", 0, 2, 1), ("ev_x", 0, 1, 1), ("ev_x", 0, 2, 0), ("tr_x", 1, 0, 0), ("load", "zs"),
    ("ev_x", 1, 0, 0), ("load", "z", 1), ("q_z", 0), ("tr_x", 1, 0, 1), ("q_x", 0, 1), ("mx", 0, 0, 0, 0),
    ("mx", 0, 0, 1, 0), ("ev_x", 0, 2, 1), ("ev_x", 1, 0, 1), ("perm_w", 0, 0), ("mx", 0, 0, 2, 0), ("q_x", 0, 2),
    ("tr_x", 1, 1, 0), ("ic_cast",), ("tr_x", 1, 1, 1), ("mx", 0, 0, 3, 0), ("perm_s", 0), ("prod", 1, 0),
    ("mx", 0, 0, 0, 1), ("exp_table",), ("prod", 1, 1), ("ev_x", 1, 1, 0), ("mx", 0, 0, 1, 1), ("ev_x", 1, 1, 1),
    ("tr_x", 1, 2, 0), ("perm_w", 0, 1), ("prod", 1, 2), ("tr_z", 1, 0), ("load", "z", 2), ("mx", 0, 0, 2, 1),
    ("mx", 0, 0, 3, 1), ("mx", 0, 0, 0, 2), ("mx", 0, 0, 1, 2), ("prod", 1, 3), ("q_x", 1, 0), ("load", "zw", 1),
    ("mx", 0, 0, 2, 2), ("perm_s", 1), ("mx", 0, 0, 3, 2), ("prod", 2, 0), ("prod", 2, 1), ("ev_x", 1, 2, 0),
    ("q_x", 1, 1), ("exp", 0, 0, 0, 0), ("tr_x", 1, 2, 1), ("ev_z", 1, 0), ("sign", 0, 0, 0, 0), ("ev_x", 1, 2, 1),
    ("tr_z", 1, 1), ("spread_t", "ic"), ("exp", 0, 0, 1, 0), ("q_x", 1, 2), ("ev_z", 1, 1), ("tr_z", 2, 0),
    ("mx", 0, 1, 0, 0), ("mx", 0, 1, 0, 1), ("mx", 0, 1, 0, 2), ("exp", 0, 0, 2, 0), ("sign", 0, 0, 1, 0), ("perm_w", 1, 0),
    ("exp", 0, 0, 3, 0), ("mx", 0, 1, 1, 0), ("q_z", 1), ("mx", 0, 1, 1, 1), ("mx", 0, 1, 1, 2), ("perm_w", 1, 1),
    ("sign", 0, 0, 2, 0), ("mx", 0, 1, 2, 0), ("ev_z", 2, 0), ("exp", 0, 1, 0, 0), ("prod", 2, 2), ("prod", 2, 3),
    ("mx", 0, 1, 2, 1), ("mx", 0, 1, 2, 2), ("exp", 0, 1, 1, 0), ("mx", 0, 1, 3, 0), ("mx", 0, 1, 3, 1), ("load", "zw", 2),
    ("load", "zw", 3), ("mx", 0, 1, 3, 2), ("mx", 1, 0, 0, 0), ("exp", 0, 1, 2, 0), ("mx", 1, 0, 0, 1), ("load", "z", 3),
    ("mx", 1, 0, 0, 2), ("sign", 0, 0, 3, 0), ("mx", 1, 0, 1, 0), ("exp", 0, 1, 3, 0), ("mx", 1, 0, 1, 1), ("sign", 0, 1, 0, 0),
    ("mx", 1, 0, 1, 2), ("prod", 3, 0), ("perm_s", 2), ("prod", 3, 1), ("mx", 1, 0, 2, 0), ("sign", 0, 1, 1, 0),
    ("sign", 0, 1, 2, 0), ("spread_v", "ic"), ("mx", 1, 0, 2, 1), ("mx", 1, 0, 2, 2), ("exp", 1, 0, 0, 0), ("mx", 1, 0, 3, 0),
    ("tr_z", 2, 1), ("tr_z", 3, 0), ("perm_w", 2, 0), ("il_v", 0, 0, 0), ("mx", 1, 0, 3, 1), ("il_s", 0, 0, 0),
    ("mx", 1, 0, 3, 2), ("sign", 0, 1, 3, 0), ("mx", 1, 1, 0, 0), ("exp", 1, 0, 1, 0), ("exp", 1, 0, 2, 0), ("mx", 1, 1, 0, 1),
    ("mx", 1, 1, 0, 2), ("mx", 1, 1, 1, 0), ("sign", 1, 0, 0, 0), ("mx", 1, 1, 1, 1), ("perm_w", 2, 1), ("mx", 1, 1, 1, 2),
    ("ev_z", 2, 1), ("perm_w", 3, 0), ("mx", 1, 1, 2, 0), ("sign", 1, 0, 1, 0), ("il_v", 0, 1, 0), ("mx", 1, 1, 2, 1),
    ("perm_w", 3, 1), ("ev_z", 3, 0), ("load", "cs"), ("mx", 1, 1, 2, 2), ("exp", 1, 0, 3, 0), ("exp", 1, 1, 0, 0),
    ("exp", 1, 1, 1, 0), ("q_z", 2), ("q_h", 0, 0, 0), ("sign", 1, 0, 2, 0), ("mx", 1, 1, 3, 0), ("prod", 3, 2),
    ("mx", 1, 1, 3, 1), ("perm_s", 3), ("mx", 1, 1, 3, 2), ("mx", 2, 0, 0, 0), ("exp", 1, 1, 2, 0), ("sign", 1, 0, 3, 0),
    ("mx", 2, 0, 0, 1), ("exp", 1, 1, 3, 0), ("mx", 2, 0, 0, 2), ("mx", 2, 0, 1, 0), ("exp", 2, 0, 0, 0), ("sign", 1, 1, 0, 0),
    ("mx", 2, 0, 1, 1), ("mx", 2, 0, 1, 2), ("prod", 3, 3), ("il_s", 0, 1, 0), ("sign", 1, 1, 1, 0), ("il_v", 1, 0, 0),
    ("sign", 1, 1, 2, 0), ("mx", 2, 0, 2, 0), ("mx", 2, 0, 2, 1), ("mx", 2, 0, 2, 2), ("mx", 2, 0, 3, 0), ("mx", 2, 0, 3, 1),
    ("q_h", 0, 1, 0), ("mx", 2, 0, 3, 2), ("tr_z", 3, 1), ("sign", 1, 1, 3, 0), ("mx", 2, 1, 0, 0), ("il_s", 1, 0, 0),
    ("exp", 2, 0, 1, 0), ("sign", 2, 0, 0, 0), ("mx", 2, 1, 0, 1), ("mx", 2, 1, 0, 2), ("mx", 2, 1, 1, 0), ("sign", 2, 0, 1, 0),
    ("load", "cw"), ("mx", 2, 1, 1, 1), ("q_h", 1, 0, 0), ("exp", 2, 0, 2, 0), ("exp", 2, 0, 3, 0), ("mx", 2, 1, 1, 2),
    ("ev_z", 3, 1), ("exp", 2, 1, 0, 0), ("sign", 2, 0, 2, 0), ("mx", 2, 1, 2, 0), ("mx", 2, 1, 2, 1), ("q_z", 3),
    ("mx", 2, 1, 2, 2), ("exp", 2, 1, 1, 0), ("sign", 2, 0, 3, 0), ("mx", 2, 1, 3, 0), ("exp", 2, 1, 2, 0), ("sign", 2, 1, 0, 0),
    ("il_v", 1, 1, 0), ("mx", 2, 1, 3, 1), ("il_v", 2, 0, 0), ("sign", 2, 1, 1, 0), ("mx", 2, 1, 3, 2), ("sign", 2, 1, 2, 0),
    ("mx", 3, 0, 0, 0), ("il_s", 1, 1, 0), ("mx", 3, 0, 0, 1), ("mx", 3, 0, 0, 2), ("exp", 2, 1, 3, 0), ("sign", 2, 1, 3, 0),
    ("mx", 3, 0, 1, 0), ("q_h", 1, 1, 0), ("exp", 3, 0, 0, 0), ("mx", 3, 0, 1, 1), ("mx", 3, 0, 1, 2), ("exp", 3, 0, 1, 0),
    ("mx", 3, 0, 2, 0), ("sign", 3, 0, 0, 0), ("mx", 3, 0, 2, 1), ("mx", 3, 0, 2, 2), ("mx", 3, 0, 3, 0), ("mx", 3, 0, 3, 1),
    ("mx", 3, 0, 3, 2), ("il_s", 2, 0, 0), ("sign", 3, 0, 1, 0), ("exp", 3, 0, 2, 0), ("mx", 3, 1, 0, 0), ("q_h", 2, 0, 0),
    ("exp", 3, 0, 3, 0), ("mx", 3, 1, 0, 1), ("mx2", 0, 0, 0), ("mx", 3, 1, 0, 2), ("mx2", 0, 0, 1), ("il_s", 2, 1, 0),
    ("sign", 3, 0, 2, 0), ("mx", 3, 1, 1, 0), ("il_v", 2, 1, 0), ("mx", 3, 1, 1, 1), ("exp", 3, 1, 0, 0), ("mx", 3, 1, 1, 2),
    ("sign", 3, 0, 3, 0), ("il_v", 3, 0, 0), ("mx2", 0, 0, 2), ("il_s", 3, 0, 0), ("mx", 3, 1, 2, 0), ("sign", 3, 1, 0, 0),
    ("exp", 3, 1, 0, 1), ("mx", 3, 1, 2, 1), ("mx", 3, 1, 2, 2), ("q_h", 3, 0, 0), ("exp", 3, 1, 1, 0), ("mx", 3, 1, 3, 0),
    ("sign", 3, 1, 0, 1), ("mx", 3, 1, 3, 1), ("exp", 3, 1, 1, 1), ("sign", 3, 1, 1, 0), ("mx2", 0, 0, 3), ("sign", 3, 1, 1, 1),
    ("mx", 3, 1, 3, 2), ("exp", 3, 1, 2, 0), ("sign", 3, 1, 2, 0), ("exp", 3, 1, 2, 1), ("mx2", 0, 1, 0), ("finish", 0, 0),
    ("q_h", 2, 1, 0), ("mx2", 0, 1, 1), ("mx2", 0, 1, 2), ("exp", 3, 1, 3, 0), ("sign", 3, 1, 2, 1), ("mx2", 0, 1, 3),
    ("sign", 3, 1, 3, 0), ("mx2", 0, 2, 0), ("mx2", 0, 2, 1), ("mx2", 0, 2, 2), ("exp", 3, 1, 3, 1), ("mx2", 0, 2, 3),
    ("il_s", 3, 1, 0), ("mx2", 0, 3, 0), ("mx2", 0, 3, 1), ("finish", 0, 1), ("il_v", 3, 1, 0), ("finish", 0, 2),
    ("sign", 3, 1, 3, 1), ("mx2", 0, 3, 2), ("mx2", 0, 3, 3), ("mx2", 1, 3, 0), ("mx2", 1, 0, 0), ("il_s", 3, 1, 1),
    ("mx2", 1, 2, 0), ("finish", 0, 3), ("mx2", 1, 0, 1), ("mx2", 1, 3, 1), ("il_v", 3, 1, 1), ("mx2", 1, 1, 0),
    ("q_h", 3, 1, 0), ("mx2", 1, 0, 2), ("mx2", 1, 1, 1), ("q_h", 3, 1, 1), ("mx2", 1, 0, 3), ("finish", 1, 0),
    ("mx2", 1, 1, 2), ("mx2", 1, 1, 3), ("finish", 1, 1), ("mx2", 1, 2, 1), ("mx2", 1, 2, 2), ("mx2", 1, 2, 3),
    ("mx2", 1, 3, 2), ("mx2", 1, 3, 3), ("finish", 1, 2), ("finish", 1, 3),
]


def tile_landmark_kernel_ridge_s3_kernel(
    tc, x_top, x_rest, z_top_bytes, z_top_scale, z_rest_words, z_rest_scales,
    landmark_gain, query_gain, alpha_words, alpha_scales, intercept, out,
):
    nc = tc.nc
    with ExitStack() as ctx:
        keep = ctx.enter_context(tc.tile_pool(name="keep", bufs=1))
        psum = ctx.enter_context(tc.psum_pool(name="psum", bufs=4))

        def alloc(name, shape, dtype, bufs=1):
            return keep.tile(shape, dtype, name=name, bufs=bufs, align_bytes=64)

        def bank(name):
            return psum.tile([P, 512], F32, name=name)

        ctx.enter_context(tc.manual_schedule())

        sc4 = alloc("sc4", [P, 4], F32)
        gain = alloc("gain", [P, NC, 4], BF16)
        qg = alloc("qg", [P, 8], BF16)
        ic4 = alloc("ic4", [P, 4], BF16)
        nc.scalar.dma_start(out=sc4[:], in_=z_top_scale.rearrange("o (p q) -> p (o q)", q=4))
        nc.scalar.dma_start(out=gain[:], in_=landmark_gain.rearrange("(c j t) -> j c t", c=NC, t=4))
        nc.gpsimd.dma_start(out=qg[:], in_=query_gain.rearrange("(p i) -> p i", i=8))
        nc.gpsimd.dma_start(out=ic4[:], in_=intercept.rearrange("(p q) -> p q", q=4))
        ident = alloc("ident", [P, P], F32)
        make_identity(nc, ident[:])
        one = alloc("one", [P, 1], F32)
        nc.vector.memset(one[:], 1.0)

        zs_raw = alloc("zs_raw", [P, 2, L], U8)
        cs = alloc("cs", [P, NC, R], U8)
        nc.vector.memset(zs_raw[:].bitcast(I32), 0)
        nc.vector.memset(cs[:].bitcast(I32), 0)

        x_top_v = x_top.rearrange("(p i) k -> p i k", i=8)
        x_rest_v = x_rest.rearrange("(p i) k -> p i k", i=8)
        zb_v = z_top_bytes.rearrange("(c j t) k -> c j t k", c=NC, t=4)
        zw_v = z_rest_words.rearrange("g p w -> p g w")

        xt = [alloc(f"xt{h}", [P, RT, A], BF16) for h in range(NH)]
        xr = [alloc(f"xr{h}", [P, RT, B], BF16) for h in range(NH)]
        zb = [alloc(f"zb{c}", [P, 4, A], U8) for c in range(NC)]
        zw_raw = [alloc(f"zw_raw{c}", [P, 2, 1024], U8) for c in range(NC)]
        cw = alloc("cw", [P, NC, 2 * R], U8)

        def load_z(c):
            nc.sync.dma_start(out=zb[c][:], in_=zb_v[c])

        def load_zw(c):
            nc.sync.dma_start(out=zw_raw[c][:], in_=zw_v[:, :, 1024 * c : 1024 * (c + 1)])

        def load_x(dst, src, h, lo=0, hi=RT):
            nc.sync.dma_start(out=dst[h][:, lo:hi, :], in_=src[:, RT * h + lo : RT * h + hi, :])

        def load_scales(dst, src):
            for q in range(4):
                nc.sync.dma_start(
                    out=dst[32 * q : 32 * q + 4, :, :].bitcast(I32),
                    in_=src[:, 4 * q : 4 * q + 4, :].rearrange("g q n -> q g n").bitcast(I32),
                )

        def load(what, *args):
            if what == "z":
                load_z(*args)
            elif what == "zw":
                load_zw(*args)
            elif what == "xt":
                load_x(xt, x_top_v, *args)
            elif what == "xr":
                load_x(xr, x_rest_v, *args)
            elif what == "zs":
                load_scales(zs_raw, z_rest_scales)
            elif what == "cs":
                load_scales(cs, alpha_scales)
            else:
                nc.sync.dma_start(out=cw[:], in_=alpha_words.rearrange("g p w -> p g w"))

        banks = {}
        grouped = {}
        junk = alloc("junk", [P, 2], F32)
        gabs = alloc("gabs", [P, NC * 4], F32)
        gclip = alloc("gclip", [P, NC * 4], F32)
        gln = alloc("gln", [P, NC * 4], F32)
        ginv = alloc("ginv", [P, NC * 4], F32)
        gsign = alloc("gsign", [P, NC * 4], F32)
        gain2 = gain[:].rearrange("p c t -> p (c t)")
        def ln_table():
            nc.scalar.activation(out=junk[:, 0:1], in_=one[:], func=ACT.Ln)

        def gain_clip():
            nc.vector.scalar_tensor_tensor(out=gabs[:], in0=gain2, scalar=-1.0, in1=gain2, op0=ALU.mult, op1=ALU.max)
            nc.vector.tensor_scalar(gclip[:], gabs[:], 2.0**-60, 2.0**60, op0=ALU.max, op1=ALU.min)

        def gain_ln():
            nc.scalar.activation(out=gln[:], in_=gclip[:], func=ACT.Ln)

        scale_row = alloc("scale_row", [P, 512], F32)
        ic_row = alloc("ic_row", [P, R], F32)
        ic4f = alloc("ic4f", [P, 4], F32)

        def ic_cast():
            nc.vector.tensor_copy(out=ic4f[:], in_=ic4[:])

        def spread_t(which):
            col4 = sc4 if which == "scale" else ic4f
            ps = bank("m")
            ps3 = ps[:].rearrange("p (q a) -> p q a", q=4)
            for q in range(4):
                nc.tensor.transpose(ps3[:, q, :], col4[:, q : q + 1].to_broadcast([P, P]), ident[:])
            banks[which] = ps3

        def spread_v(which):
            row = scale_row if which == "scale" else ic_row
            nc.vector.tensor_copy(out=row[:].rearrange("p (a q) -> p a q", q=4), in_=banks[which].rearrange("p q a -> p a q"))

        xq = [[alloc(f"xq{h}_{g}", [P, MH], U32) for g in range(3)] for h in range(NH)]
        xs = [[alloc(f"xs{h}_{g}", [P, MH], U8) for g in range(3)] for h in range(NH)]
        def turn(key, sources):
            ps = bank("m")
            ps4 = ps[:].rearrange("p (s u r) -> p s u r", s=2, u=2)
            for s, src in enumerate(sources):
                words = src.bitcast(F32)
                for u in range(2):
                    nc.tensor.transpose(ps4[:, s, u, :], words[:, u : 256 : 2], ident[:])
            banks[key] = ps4

        def emit_out(key, dst, half, engine_copy):
            flat = dst[:].rearrange("p m t -> p (m t)").bitcast(F32)
            engine_copy(
                out=flat[:, 512 * half : 512 * half + 512].rearrange("p (s r u) -> p s r u", s=2, u=2),
                in_=banks[key].rearrange("p s u r -> p s r u"),
            )

        def x_source(h, g, rt):
            if g == 0:
                return xt[h][:, rt, :]
            return xr[h][:, rt, 512 * (g - 1) : 512 * g]

        def tr_x(h, g, b):
            turn(("x", h, g, b), [x_source(h, g, 2 * b), x_source(h, g, 2 * b + 1)])

        def ev_x(h, g, b):
            engine_copy = nc.vector.tensor_copy if ("x", h, g, b) in EV_VECTOR else nc.scalar.copy
            if ("x", h, g) not in grouped:
                grouped["x", h, g] = alloc("xg", [P, MH, 4], BF16, bufs=4)
            emit_out(("x", h, g, b), grouped["x", h, g], b, engine_copy)

        def q_x(h, g):
            nc.vector.quantize_mx(out=xq[h][g][:].bitcast(FP8X4), scales=xs[h][g][:], in_=grouped["x", h, g][:].rearrange("p m t -> p (m t)"))

        zq = [alloc(f"zq{c}", [P, 512], U32) for c in range(NC)]
        zqs = [alloc(f"zqs{c}", [P, 512], U8) for c in range(NC)]
        zw = [alloc(f"zw{c}", [P, 2, 1024], U8) for c in range(NC)]
        zs = [alloc(f"zs{c}", [P, 2, 512], U8) for c in range(NC)]
        zf = {}

        def prod(c, t):
            if c not in zf:
                zf[c] = alloc("zf", [P, 4, A], BF16, bufs=3)
            nc.vector.tensor_tensor(out=zf[c][:, t, :], in0=zb[c][:, t, :].bitcast(FP8), in1=scale_row[:], op=ALU.mult)

        def perm_s(c):
            nc.vector.tensor_copy(
                out=zs[c][:].rearrange("p g (t j) -> p g t j", t=4),
                in_=zs_raw[:, :, 512 * c : 512 * (c + 1)].rearrange("p g (j t) -> p g t j", t=4),
            )

        def perm_w(c, g):
            nc.vector.tensor_copy(
                out=zw[c][:, g, :].rearrange("p (t j b) -> p t j b", t=4, b=2),
                in_=zw_raw[c][:, g, :].rearrange("p (j t b) -> p t j b", t=4, b=2),
            )

        def tr_z(c, b):
            turn(("z", c, b), [zf[c][:, 2 * b, :], zf[c][:, 2 * b + 1, :]])

        def ev_z(c, b):
            engine_copy = nc.vector.tensor_copy if ("z", c, b) in EV_VECTOR else nc.scalar.copy
            if ("z", c) not in grouped:
                grouped["z", c] = alloc("zg", [P, 512, 4], BF16, bufs=3)
            emit_out(("z", c, b), grouped["z", c], b, engine_copy)

        def q_z(c):
            nc.vector.quantize_mx(out=zq[c][:].bitcast(FP8X4), scales=zqs[c][:], in_=grouped["z", c][:].rearrange("p m t -> p (m t)"))

        hq = [[alloc(f"hq{h}_{c}", [P, MH], U32) for c in range(NC)] for h in range(NH)]
        hqs = [[alloc(f"hqs{h}_{c}", [P, MH], U8) for c in range(NC)] for h in range(NH)]
        planes = {}

        def mx(c, h, t, g):
            order = PASSES[c, h]
            if g == order[0]:
                banks["u", c, h, t] = bank("u")
            if g == 0:
                lhs = zq[c][:, P * t : P * (t + 1)].bitcast(FP8X4)
                lhs_scale = zqs[c][:, P * t : P * (t + 1)]
            else:
                lhs = zw[c][:, g - 1, 2 * P * t : 2 * P * (t + 1)].bitcast(FP4X4)
                lhs_scale = zs[c][:, g - 1, P * t : P * (t + 1)]
            nc.tensor.matmul_mx(
                out=banks["u", c, h, t][:], lhsT=lhs, lhsT_scale=lhs_scale,
                rhs=xq[h][g][:].bitcast(FP8X4), rhs_scale=xs[h][g][:],
                start=(g == order[0]), stop=(g == order[2]),
            )

        def exp(c, h, t, part=0):
            lo, cut, hi = CUTS[c, h][part]
            if ("hp", c, h) not in planes:
                planes["hp", c, h] = alloc("hp", [P, 4, MH], BF16, bufs=3)
                planes["hs", c, h] = alloc("hs", [P, 4, MH], BF16, bufs=3)
                planes["hg", c, h] = alloc("hg", [P, MH, 4], BF16, bufs=3)
            i = 4 * c + t
            nc.scalar.activation(out=planes["hp", c, h][:, t, lo:hi], in_=banks["u", c, h, t][:, lo:hi], func=ACT.Exp, bias=gln[:, i : i + 1])

        def sign(c, h, t, part=0):
            lo, cut, hi = CUTS[c, h][part]
            i = 4 * c + t
            nc.vector.tensor_scalar(planes["hs", c, h][:, t, lo:hi], planes["hp", c, h][:, t, lo:hi], gsign[:, i : i + 1], None, op0=ALU.mult)

        def il(c, h, engine_copy, lo, hi):
            engine_copy(
                out=planes["hg", c, h][:, lo:hi, :].rearrange("p (e i) t -> p e t i", i=4),
                in_=planes["hs", c, h][:, :, lo:hi].rearrange("p t (e i) -> p e t i", i=4),
            )

        def il_s(c, h, part=0):
            lo, cut, hi = CUTS[c, h][part]
            il(c, h, nc.scalar.copy, lo, cut)

        def il_v(c, h, part=0):
            lo, cut, hi = CUTS[c, h][part]
            il(c, h, nc.vector.tensor_copy, cut, hi)

        def q_h(c, h, part=0):
            lo, cut, hi = CUTS[c, h][part]
            nc.vector.quantize_mx(
                out=hq[h][c][:, lo:hi].bitcast(FP8X4), scales=hqs[h][c][:, lo:hi],
                in_=planes["hg", c, h][:, lo:hi, :].rearrange("p m t -> p (m t)"),
            )

        out_v = out.rearrange("(p i) r -> p i r", i=8)

        def mx2(h, rt, c):
            if c == 0:
                banks["o", h, rt] = bank("m")
            cols = slice(P * rt, P * (rt + 1))
            nc.tensor.matmul_mx(
                out=banks["o", h, rt][:], lhsT=hq[h][c][:, cols].bitcast(FP8X4), lhsT_scale=hqs[h][c][:, cols],
                rhs=cw[:, c, :].bitcast(FP4X4), rhs_scale=cs[:, c, :],
                start=(c == 0), stop=(c == NC - 1),
            )

        def finish(h, rt):
            i = RT * h + rt
            res = alloc("res", [P, R], F32, bufs=4)
            nc.vector.scalar_tensor_tensor(out=res[:], in0=banks["o", h, rt][:], scalar=qg[:, i : i + 1], in1=ic_row[:], op0=ALU.mult, op1=ALU.add)
            nc.sync.dma_start(out=out_v[:, i, :], in_=res[:])

        def gain_sign():
            nc.vector.reciprocal(out=ginv[:], in_=gclip[:])
            nc.vector.tensor_tensor(out=gsign[:], in0=gain2, in1=ginv[:], op=ALU.mult)

        def exp_table():
            nc.scalar.activation(out=junk[:, 1:2], in_=gln[:, 0:1], func=ACT.Exp)

        jobs = dict(load=load, ic_cast=ic_cast, ln_table=ln_table, gain_clip=gain_clip, gain_ln=gain_ln, gain_sign=gain_sign, exp_table=exp_table, spread_t=spread_t, spread_v=spread_v,
                    tr_x=tr_x, ev_x=ev_x, q_x=q_x, prod=prod, perm_s=perm_s, perm_w=perm_w, tr_z=tr_z, ev_z=ev_z, q_z=q_z, mx=mx, exp=exp, sign=sign,
                    il_s=il_s, il_v=il_v, q_h=q_h, mx2=mx2, finish=finish)
        for name, *args in ORDER:
            jobs[name](*args)
